import numpy as np
import ml_dtypes


def mxq(x, axis, fmt="e4m3"):
    dtype, down = {"e4m3": (ml_dtypes.float8_e4m3fn, 7), "e5m2": (ml_dtypes.float8_e5m2, 14)}[fmt]
    v = np.moveaxis(np.asarray(x, np.float32).astype(ml_dtypes.bfloat16).astype(np.float64), axis, -1)
    blocks = v.reshape(v.shape[:-1] + (-1, 32))
    amax = np.abs(blocks).max(-1, keepdims=True)
    byte = np.maximum(np.where(amax > 0, np.frexp(amax)[1] - 1 + 127, 0) - down, 1)
    scale = np.exp2(byte - 127.0)
    codes = (blocks / scale).astype(np.float32).astype(dtype).astype(np.float64)
    return np.moveaxis((codes * scale).reshape(v.shape), -1, axis)


WIDE = False


def mx_kscale(k):
    if not WIDE:
        return np.ones(k)
    levels = np.array([10, -10, 5, -5, 0])
    if k % 512:
        return np.exp2(np.random.permutation(np.resize(levels, k // 32))).repeat(32)
    a = np.empty((k // 512, 16))
    for p in range(k // 512):
        a[p, :8] = np.random.permutation(np.resize(levels, 8))
        for g in range(8):
            far = levels[np.abs(levels - a[p, g]) >= 10]
            a[p, g + 8] = far[np.random.randint(len(far))]
    return np.exp2(a.ravel()).repeat(32)


def f64(x):
    return np.asarray(x).astype(np.float64)


def planes(y):
    n, m = y.shape
    v = y.astype(np.float32).astype(ml_dtypes.bfloat16).astype(np.float64).reshape(n // 32, 32, m)
    top = np.abs(v).max(1)
    byte = np.clip(np.where(top > 0, np.frexp(top)[1] - 1 + 127 - 7, 1), 1, 254)
    codes = (v * np.exp2(127.0 - byte)[:, None, :]).reshape(n, m).astype(np.float32).astype(ml_dtypes.float8_e4m3fn).view(np.uint8)
    words = codes.reshape(n // 512, 128, 4, m).transpose(0, 1, 3, 2)
    return np.ascontiguousarray(words), np.ascontiguousarray(byte.astype(np.uint8).reshape(n // 512, 16, m))


def split(x):
    m, e = np.frexp(f64(x))
    hi = np.ldexp(np.trunc(16.0 * m) / 16.0, e)
    return hi, f64(x) - hi


K, M, T = 1024, 1024, 1024


def setup_inputs():
    n = np.random.standard_normal
    s = mx_kscale(K)[:, None]
    return {
        "w": (n((K, M)) / np.sqrt(K) / s).astype(np.float32),
        "x": (n((K, T)) * s).astype(np.float32),
    }


def reference(w, x):
    w_hi, w_lo = split(w)
    w_hi_, w_lo_ = mxq(w_hi, 0, "e4m3"), mxq(w_lo, 0, "e4m3")
    x_ = mxq(f64(x), 0, "e4m3")
    y = x_.T @ w_hi_ + x_.T @ w_lo_
    out_0 = np.maximum(y, 0.0) ** 2
    return (out_0,) + planes(out_0)

@@ -1,0 +1,162 @@
+from contextlib import ExitStack
+
+import concourse.mybir as mybir
+
+K, M, T = 1024, 1024, 1024
+FLOPS = 2 * 2 * K * M * T
+
+F32 = mybir.dt.float32
+BF16 = mybir.dt.bfloat16
+I32 = mybir.dt.int32
+U32 = mybir.dt.uint32
+U8 = mybir.dt.uint8
+FP8X4 = mybir.dt.float8_e4m3fn_x4
+ALU = mybir.AluOpType
+ACT = mybir.ActivationFunctionType
+
+P = 128
+CH = 256
+HI_MASK_PAIR = 0xFFF0FFF0 - (1 << 32)
+
+BANKS = [(a, h, r) for h in range(2) for a in range(2) for r in range(4)]
+
+ORDER = (
+    "Lw0_0 Lw1_01 wc00:V wm00 wl00 Lw0_1 wc01:S wc11:V Lx0_23 wq00 wh00 wm11 wc10:S wm01 wl11 wl01 Lw0_23 xc30:S "
+    "wm10 wh01 wh10 wq01 xc20:S wl10 Lx0_01 wc30:S xq10 wq10 wq11 M0_4 wc20:S wm30 Lx1_01 wh11 wl30 M0_5 xc00:S "
+    "xc10:V M0_6 xq00 M0_7 Lx1_23 wq30 M0_2 wm20 xc11:S wh30 M0_3 xc01:V M0_1 xq01 M0_0 Lw1_23 wl20 M1_3 xc31:S "
+    "M1_0 xc21:V M1_2 wh20 A3:S M1_1 wq20 A2:S xq11 M0_11 A0:S M1_5 wc21:V B3:S M1_7 wc31:V A1:S M1_6 wm21 A5:S "
+    "wm31 So003 M0_10 wh21 B1:S wl31 M1_4 B2:S M0_13 A4:S wl21 So001 M0_9 B5:S So002 M0_12 B4:S wh31 M0_8 wq21 A6:S "
+    "wq31 A7:V M1_11 B0:S So100 B6:V M1_8 B7:S So101 C00:V A11:S M1_9 C01:V A8:S M0_15 So102 C10:V B11:S M1_10 "
+    "So103 B8:V A9:S M1_13 So000 Q01 A10:S M1_12 So013 Q00 B9:S Q10 M1_15 So010 C11:V B10:S M0_14 Sw00 A13:V A12:S "
+    "M1_14 Q11 So011 B13:S A15:V So012 A14:S B12:V Sw10 B15:S C02:V B14:S So111 C03:V So110 Q02 C12:S Q03 So113 "
+    "C13:V So112 Q12 Q13 Ss0 Sw01 Sw11 Ss1 "
+).split()
+
+
+def tile_mix_hilo_tm_pl_relu2_kernel(tc, w, x, out_0, out_1, out_2):
+    nc = tc.nc
+    with ExitStack() as ctx:
+        sb = ctx.enter_context(tc.tile_pool(name="sb", bufs=1))
+        ps = ctx.enter_context(tc.psum_pool(name="ps", bufs=1))
+        ctx.enter_context(tc.manual_schedule())
+
+        def new(name, shape, dtype):
+            return sb.tile(shape, dtype, name=name, align_bytes=256)
+
+        raw = {}
+        hi = {(c, g): new("hi%d%d" % (c, g), [P, CH, 4], BF16) for c in range(4) for g in range(2)}
+        lo = {(c, g): new("lo%d%d" % (c, g), [P, CH, 4], BF16) for c in range(4) for g in range(2)}
+        xb = {(a, g): new("xb%d%d" % (a, g), [P, 4, P, 4], BF16) for a in range(2) for g in range(2)}
+        wcode = {(s, h, g): new("wcode%d%d%d" % (s, h, g), [P, 512], U32) for s in range(2) for h in range(2) for g in range(2)}
+        wscale = {(s, h, g): new("wscale%d%d%d" % (s, h, g), [P, 512], U8) for s in range(2) for h in range(2) for g in range(2)}
+        xcode = {(a, g): new("xcode%d%d" % (a, g), [P, 512], U32) for a in range(2) for g in range(2)}
+        xscale = {(a, g): new("xscale%d%d" % (a, g), [P, 512], U8) for a in range(2) for g in range(2)}
+        res = {(a, h): new("res%d%d" % (a, h), [P, 4, 512], F32) for a in range(2) for h in range(2)}
+        ob = {(a, c): new("ob%d%d" % (a, c), [P, CH, 4], BF16) for a in range(2) for c in range(4)}
+        ocode = {(a, h): new("ocode%d%d" % (a, h), [P, 512], U32) for a in range(2) for h in range(2)}
+        oscale = {a: new("oscale%d" % a, [P, M], U8) for a in range(2)}
+        bank = [ps.tile([P, 512], F32, name="bank%d" % i) for i in range(8)]
+
+        warm = new("warm", [P, 8], F32)
+        nc.vector.memset(warm[:], 0.0)
+        nc.scalar.activation(out=warm[:], in_=warm[:], func=ACT.Square)
+
+        def copy(eng, out, in_):
+            if eng == "V":
+                nc.vector.tensor_copy(out=out, in_=in_)
+            else:
+                nc.scalar.copy(out=out, in_=in_)
+
+        def quant(codes, scales, src):
+            nc.vector.quantize_mx(out=codes.bitcast(FP8X4), scales=scales, in_=src)
+
+        def flat(t):
+            return t[:].rearrange("p n j -> p (n j)")
+
+        def by_runs(t):
+            return t[:].rearrange("p (c i) j -> p c j i", i=4)
+
+        out_rows = out_0.rearrange("(a p r) n -> a p r n", a=2, r=4)
+        words_out = out_1.rearrange("a p n i -> a p (n i)").bitcast(I32)
+        scales_out = out_2.bitcast(I32)
+
+        for step in ORDER:
+            name, eng = (step.split(":") + [""])[:2]
+            if name[0] == "L":
+                src = w if name[1] == "w" else x
+                g = int(name[2])
+                cs = [int(ch) for ch in name[4:]]
+                t = new("raw" + name, [P, 4, CH * len(cs)], F32)
+                rows = src[512 * g : 512 * (g + 1), CH * cs[0] : CH * (cs[-1] + 1)]
+                nc.sync.dma_start(out=t[:], in_=rows.rearrange("(p j) n -> p j n", j=4))
+                for i, c in enumerate(cs):
+                    raw[(name[1], c, g)] = (t, CH * i)
+            elif name[0] in "wx" and name[:2] != "xq":
+                c, g = int(name[2]), int(name[3])
+                t, c0 = raw[(name[0], c, g)]
+                cols = slice(CH * (c % 2), CH * (c % 2 + 1))
+                if name[:2] == "wc":
+                    upper = t[:].bitcast(BF16)[:, :, 2 * c0 + 1 : 2 * (c0 + CH) : 2]
+                    copy(eng, by_runs(hi[(c, g)]), upper.rearrange("p j (c i) -> p c j i", i=4))
+                elif name[:2] == "wm":
+                    v = flat(hi[(c, g)]).bitcast(I32)
+                    nc.vector.tensor_scalar(out=v, in0=v, scalar1=HI_MASK_PAIR, scalar2=None, op0=ALU.bitwise_and)
+                elif name[:2] == "wl":
+                    nc.vector.tensor_tensor(
+                        out=by_runs(lo[(c, g)]),
+                        in0=t[:, :, c0 : c0 + CH].rearrange("p j (c i) -> p c j i", i=4),
+                        in1=by_runs(hi[(c, g)]),
+                        op=ALU.subtract,
+                    )
+                elif name[:2] == "wh":
+                    quant(wcode[(0, c // 2, g)][:, cols], wscale[(0, c // 2, g)][:, cols], flat(hi[(c, g)]))
+                elif name[:2] == "wq":
+                    quant(wcode[(1, c // 2, g)][:, cols], wscale[(1, c // 2, g)][:, cols], flat(lo[(c, g)]))
+                else:
+                    dst = xb[(c // 2, g)][:, :, 64 * (c % 2) : 64 * (c % 2 + 1), :].rearrange("p r m j -> p m j r")
+                    copy(eng, dst, t[:, :, c0 : c0 + CH].rearrange("p j (m r) -> p m j r", r=4))
+            elif name[:2] == "xq":
+                a, g = int(name[2]), int(name[3])
+                quant(xcode[(a, g)][:], xscale[(a, g)][:], xb[(a, g)][:].rearrange("p r m j -> p (r m j)"))
+            elif name[0] == "M":
+                g, k = int(name[1]), int(name[3:])
+                a, h, r = BANKS[k]
+                for s in range(2):
+                    nc.tensor.matmul_mx(
+                        out=bank[k % 8][:],
+                        lhsT=xcode[(a, g)][:, P * r : P * (r + 1)].bitcast(FP8X4),
+                        lhsT_scale=xscale[(a, g)][:, P * r : P * (r + 1)],
+                        rhs=wcode[(s, h, g)][:].bitcast(FP8X4),
+                        rhs_scale=wscale[(s, h, g)][:],
+                        start=(g == 0 and s == 0),
+                        stop=(g == 1 and s == 1),
+                    )
+            elif name[0] in "AB":
+                k = int(name[1:])
+                a, h, r = BANKS[k]
+                dst = res[(a, h)][:, r, :]
+                if name[0] == "A" and eng == "V":
+                    nc.vector.tensor_scalar(out=dst, in0=bank[k % 8][:], scalar1=0.0, scalar2=None, op0=ALU.max)
+                elif name[0] == "A":
+                    nc.scalar.activation(out=dst, in_=bank[k % 8][:], func=ACT.Relu)
+                elif eng == "V":
+                    nc.vector.tensor_tensor(out=dst, in0=dst, in1=dst, op=ALU.mult)
+                else:
+                    nc.scalar.activation(out=dst, in_=dst, func=ACT.Square)
+            elif name[0] in "CQ":
+                a, c = int(name[1]), int(name[2])
+                cols = slice(CH * (c % 2), CH * (c % 2 + 1))
+                if name[0] == "C":
+                    copy(eng, by_runs(ob[(a, c)]), res[(a, c // 2)][:, :, cols].rearrange("p r (c i) -> p c r i", i=4))
+                else:
+                    quant(ocode[(a, c // 2)][:, cols], oscale[a][:, CH * c : CH * (c + 1)], flat(ob[(a, c)]))
+            elif name[:2] == "So":
+                a, h, r = int(name[2]), int(name[3]), int(name[4])
+                nc.sync.dma_start(out=out_rows[a, :, r, 512 * h : 512 * (h + 1)], in_=res[(a, h)][:, r, :])
+            elif name[:2] == "Sw":
+                a, h = int(name[2]), int(name[3])
+                nc.sync.dma_start(out=words_out[a, :, 512 * h : 512 * (h + 1)], in_=ocode[(a, h)][:].bitcast(I32))
+            else:
+                a = int(name[2])
+                for q in range(4):
+                    nc.sync.dma_start(out=scales_out[a, 4 * q : 4 * q + 4, :], in_=oscale[a][32 * q : 32 * q + 4, :].bitcast(I32))

@@ -74,7 +74,7 @@ def tile_mix_hilo_tm_pl_relu2_kernel(tc, w, x, out_0, out_1, out_2):
             return t[:].rearrange("p n j -> p (n j)")
 
         def by_runs(t):
-            return t[:].rearrange("p (c i) j -> p c j i", i=4)
+            return t[:].rearrange("p (c i) j -> p c j i", i=2)
 
         out_rows = out_0.rearrange("(a p r) n -> a p r n", a=2, r=4)
         words_out = out_1.rearrange("a p n i -> a p (n i)").bitcast(I32)
@@ -97,14 +97,14 @@ def tile_mix_hilo_tm_pl_relu2_kernel(tc, w, x, out_0, out_1, out_2):
                 cols = slice(CH * (c % 2), CH * (c % 2 + 1))
                 if name[:2] == "wc":
                     upper = t[:].bitcast(BF16)[:, :, 2 * c0 + 1 : 2 * (c0 + CH) : 2]
-                    copy(eng, by_runs(hi[(c, g)]), upper.rearrange("p j (c i) -> p c j i", i=4))
+                    copy(eng, by_runs(hi[(c, g)]), upper.rearrange("p j (c i) -> p c j i", i=2))
                 elif name[:2] == "wm":
                     v = flat(hi[(c, g)]).bitcast(I32)
                     nc.vector.tensor_scalar(out=v, in0=v, scalar1=HI_MASK_PAIR, scalar2=None, op0=ALU.bitwise_and)
                 elif name[:2] == "wl":
                     nc.vector.tensor_tensor(
                         out=by_runs(lo[(c, g)]),
-                        in0=t[:, :, c0 : c0 + CH].rearrange("p j (c i) -> p c j i", i=4),
+                        in0=t[:, :, c0 : c0 + CH].rearrange("p j (c i) -> p c j i", i=2),
                         in1=by_runs(hi[(c, g)]),
                         op=ALU.subtract,
                     )
@@ -147,7 +147,7 @@ def tile_mix_hilo_tm_pl_relu2_kernel(tc, w, x, out_0, out_1, out_2):
                 a, c = int(name[1]), int(name[2])
                 cols = slice(CH * (c % 2), CH * (c % 2 + 1))
                 if name[0] == "C":
-                    copy(eng, by_runs(ob[(a, c)]), res[(a, c // 2)][:, :, cols].rearrange("p r (c i) -> p c r i", i=4))
+                    copy(eng, by_runs(ob[(a, c)]), res[(a, c // 2)][:, :, cols].rearrange("p r (c i) -> p c r i", i=2))
                 else:
                     quant(ocode[(a, c // 2)][:, cols], oscale[a][:, CH * c : CH * (c + 1)], flat(ob[(a, c)]))
             elif name[:2] == "So":

@@ -15,21 +15,23 @@ ALU = mybir.AluOpType
 ACT = mybir.ActivationFunctionType
 
 P = 128
-CH = 256
 HI_MASK_PAIR = 0xFFF0FFF0 - (1 << 32)
 
-BANKS = [(a, h, r) for h in range(2) for a in range(2) for r in range(4)]
+PACK = {(0, 0): 1, (0, 4): 2, (0, 6): 2, (1, 0): 1, (1, 4): 2, (1, 6): 2}
 
 ORDER = (
-    "Lw0_0 Lw1_01 wc00:V wm00 wl00 Lw0_1 wc01:S wc11:V Lx0_23 wq00 wh00 wm11 wc10:S wm01 wl11 wl01 Lw0_23 xc30:S "
-    "wm10 wh01 wh10 wq01 xc20:S wl10 Lx0_01 wc30:S xq10 wq10 wq11 M0_4 wc20:S wm30 Lx1_01 wh11 wl30 M0_5 xc00:S "
-    "xc10:V M0_6 xq00 M0_7 Lx1_23 wq30 M0_2 wm20 xc11:S wh30 M0_3 xc01:V M0_1 xq01 M0_0 Lw1_23 wl20 M1_3 xc31:S "
-    "M1_0 xc21:V M1_2 wh20 A3:S M1_1 wq20 A2:S xq11 M0_11 A0:S M1_5 wc21:V B3:S M1_7 wc31:V A1:S M1_6 wm21 A5:S "
-    "wm31 So003 M0_10 wh21 B1:S wl31 M1_4 B2:S M0_13 A4:S wl21 So001 M0_9 B5:S So002 M0_12 B4:S wh31 M0_8 wq21 A6:S "
-    "wq31 A7:V M1_11 B0:S So100 B6:V M1_8 B7:S So101 C00:V A11:S M1_9 C01:V A8:S M0_15 So102 C10:V B11:S M1_10 "
-    "So103 B8:V A9:S M1_13 So000 Q01 A10:S M1_12 So013 Q00 B9:S Q10 M1_15 So010 C11:V B10:S M0_14 Sw00 A13:V A12:S "
-    "M1_14 Q11 So011 B13:S A15:V So012 A14:S B12:V Sw10 B15:S C02:V B14:S So111 C03:V So110 Q02 C12:S Q03 So113 "
-    "C13:V So112 Q12 Q13 Ss0 Sw01 Sw11 Ss1 "
+    "Lw002 Lw022 wc002:V Lw104 wm002 wc022:S wl002 Lx044 wc102:S wm022 Lw042 wc122:S wq002 wl022 wh022 wq022 wm102 "
+    "wh002 Lx144 xc062:S wl102 wm122 wh102 wl122 xc042:S Lw142 wh122 wc042:S Lx004 xq10 M01041:0 Lx104 wq102 "
+    "xc142:S M01042:1 wm042 Lw062 wq122 xc162:V wh042 xq11 M11041:0 M11042:1 M01040:2 wc142:S wl042 A1041:S0 wm142 "
+    "A1042:S1 M11040:2 wq042 M01420:3 wh142 wl142 B10411:S Lw162 xc022:V M01043:4 wq142 xc002:S B10421:S xq00 "
+    "M11043:4 xc102:V M01422:5 xc122:V M11422:5 wc062:V xq01 wm062 M11420:3 So10421 A1040:S2 M00420:6 wc162:V "
+    "M00422:7 M00041:0 A1043:S4 B10401:S A1420:S3 M00040:1 wl062 So10411 M10041:0 wm162 So10401 wq062 B10431:S "
+    "B14202:S wh062 A1422:S5 A0041:S0 B14222:S M00042:2 B00411:S wh162 M00043:4 M10042:2 A0042:S2 So10431 So14202 "
+    "So14222 wl162 M10040:1 M00622:3 C122:V A0040:S1 M10422:7 B00421:S M10043:4 B00401:V M00620:5 wq162 M10420:6 "
+    "M01622:0 A0422:S7 C102:V M11622:0 M10620:5 A0043:S4 M01620:2 B04222:S M10622:3 A0420:V6 M11620:2 B00431:S "
+    "B04202:S Q102 So00411 C142:V A1622:S0 Q122 So00421 Q142 C042:V C022:V A0620:S5 So00401 So04222 So00431 "
+    "B16222:S A0622:V3 B06202:S B06222:S A1620:V2 B16202:S So04202 Sw106 So16222 Q022 C002:V So06202 Q042 So06222 "
+    "Q002 C162:V So16202 C062:S Sw006 Q062 Q162 Sw062 Ssm1 Ssm3:A Ssm2 Ssm0 Sw162:A "
 ).split()
 
 
@@ -43,18 +45,14 @@ def tile_mix_hilo_tm_pl_relu2_kernel(tc, w, x, out_0, out_1, out_2):
         def new(name, shape, dtype):
             return sb.tile(shape, dtype, name=name, align_bytes=256)
 
-        raw = {}
-        hi = {(c, g): new("hi%d%d" % (c, g), [P, CH, 4], BF16) for c in range(4) for g in range(2)}
-        lo = {(c, g): new("lo%d%d" % (c, g), [P, CH, 4], BF16) for c in range(4) for g in range(2)}
+        raw, hi, lo, res, ob = {}, {}, {}, {}, {}
         xb = {(a, g): new("xb%d%d" % (a, g), [P, 4, P, 4], BF16) for a in range(2) for g in range(2)}
-        wcode = {(s, h, g): new("wcode%d%d%d" % (s, h, g), [P, 512], U32) for s in range(2) for h in range(2) for g in range(2)}
-        wscale = {(s, h, g): new("wscale%d%d%d" % (s, h, g), [P, 512], U8) for s in range(2) for h in range(2) for g in range(2)}
+        wcode = {(s, g): new("wcode%d%d" % (s, g), [P, M], U32) for s in range(2) for g in range(2)}
+        wscale = {(s, g): new("wscale%d%d" % (s, g), [P, M], U8) for s in range(2) for g in range(2)}
         xcode = {(a, g): new("xcode%d%d" % (a, g), [P, 512], U32) for a in range(2) for g in range(2)}
         xscale = {(a, g): new("xscale%d%d" % (a, g), [P, 512], U8) for a in range(2) for g in range(2)}
-        res = {(a, h): new("res%d%d" % (a, h), [P, 4, 512], F32) for a in range(2) for h in range(2)}
-        ob = {(a, c): new("ob%d%d" % (a, c), [P, CH, 4], BF16) for a in range(2) for c in range(4)}
-        ocode = {(a, h): new("ocode%d%d" % (a, h), [P, 512], U32) for a in range(2) for h in range(2)}
-        oscale = {a: new("oscale%d" % a, [P, M], U8) for a in range(2)}
+        ocode = {a: new("ocode%d" % a, [P, M], U32) for a in range(2)}
+        oscale = new("oscale", [P, M], U8)
         bank = [ps.tile([P, 512], F32, name="bank%d" % i) for i in range(8)]
 
         warm = new("warm", [P, 8], F32)
@@ -81,82 +79,100 @@ def tile_mix_hilo_tm_pl_relu2_kernel(tc, w, x, out_0, out_1, out_2):
         scales_out = out_2.bitcast(I32)
 
         for step in ORDER:
-            name, eng = (step.split(":") + [""])[:2]
-            if name[0] == "L":
-                src = w if name[1] == "w" else x
-                g = int(name[2])
-                cs = [int(ch) for ch in name[4:]]
-                t = new("raw" + name, [P, 4, CH * len(cs)], F32)
-                rows = src[512 * g : 512 * (g + 1), CH * cs[0] : CH * (cs[-1] + 1)]
+            name, arg = (step.split(":") + [""])[:2]
+            kind = name[:2] if name[0] in "LwxMS" else name[0]
+            d = [int(ch) for ch in name[len(kind) :] if ch in "0123456789"]
+            queue = nc.scalar if arg == "A" else nc.sync
+            if kind[0] == "L":
+                g, c0, n = d
+                src = w if kind == "Lw" else x
+                t = new("raw" + name, [P, 4, P * n], F32)
+                rows = src[512 * g : 512 * (g + 1), P * c0 : P * (c0 + n)]
                 nc.sync.dma_start(out=t[:], in_=rows.rearrange("(p j) n -> p j n", j=4))
-                for i, c in enumerate(cs):
-                    raw[(name[1], c, g)] = (t, CH * i)
-            elif name[0] in "wx" and name[:2] != "xq":
-                c, g = int(name[2]), int(name[3])
-                t, c0 = raw[(name[0], c, g)]
-                cols = slice(CH * (c % 2), CH * (c % 2 + 1))
-                if name[:2] == "wc":
-                    upper = t[:].bitcast(BF16)[:, :, 2 * c0 + 1 : 2 * (c0 + CH) : 2]
-                    copy(eng, by_runs(hi[(c, g)]), upper.rearrange("p j (c i) -> p c j i", i=2))
-                elif name[:2] == "wm":
-                    v = flat(hi[(c, g)]).bitcast(I32)
+                for i in range(n):
+                    raw[(kind[1], g, c0 + i)] = (t, P * i)
+            elif kind in ("wc", "wm", "wl", "wh", "wq", "xc"):
+                g, c0, n = d
+                t, off = raw[(kind[0], g, c0)]
+                cols = slice(P * c0, P * (c0 + n))
+                key = (g, c0)
+                if kind == "wc":
+                    hi[key] = new("hi" + name, [P, P * n, 4], BF16)
+                    lo[key] = new("lo" + name, [P, P * n, 4], BF16)
+                    upper = t[:].bitcast(BF16)[:, :, 2 * off + 1 : 2 * (off + P * n) : 2]
+                    copy(arg, by_runs(hi[key]), upper.rearrange("p j (c i) -> p c j i", i=2))
+                elif kind == "wm":
+                    v = flat(hi[key]).bitcast(I32)
                     nc.vector.tensor_scalar(out=v, in0=v, scalar1=HI_MASK_PAIR, scalar2=None, op0=ALU.bitwise_and)
-                elif name[:2] == "wl":
+                elif kind == "wl":
                     nc.vector.tensor_tensor(
-                        out=by_runs(lo[(c, g)]),
-                        in0=t[:, :, c0 : c0 + CH].rearrange("p j (c i) -> p c j i", i=2),
-                        in1=by_runs(hi[(c, g)]),
+                        out=by_runs(lo[key]),
+                        in0=t[:, :, off : off + P * n].rearrange("p j (c i) -> p c j i", i=2),
+                        in1=by_runs(hi[key]),
                         op=ALU.subtract,
                     )
-                elif name[:2] == "wh":
-                    quant(wcode[(0, c // 2, g)][:, cols], wscale[(0, c // 2, g)][:, cols], flat(hi[(c, g)]))
-                elif name[:2] == "wq":
-                    quant(wcode[(1, c // 2, g)][:, cols], wscale[(1, c // 2, g)][:, cols], flat(lo[(c, g)]))
+                elif kind == "wh":
+                    quant(wcode[(0, g)][:, cols], wscale[(0, g)][:, cols], flat(hi[key]))
+                elif kind == "wq":
+                    quant(wcode[(1, g)][:, cols], wscale[(1, g)][:, cols], flat(lo[key]))
                 else:
-                    dst = xb[(c // 2, g)][:, :, 64 * (c % 2) : 64 * (c % 2 + 1), :].rearrange("p r m j -> p m j r")
-                    copy(eng, dst, t[:, :, c0 : c0 + CH].rearrange("p j (m r) -> p m j r", r=4))
-            elif name[:2] == "xq":
-                a, g = int(name[2]), int(name[3])
+                    m0 = 32 * (c0 % 4)
+                    dst = xb[(c0 // 4, g)][:, :, m0 : m0 + 32 * n, :].rearrange("p r m j -> p m j r")
+                    copy(arg, dst, t[:, :, off : off + P * n].rearrange("p j (m r) -> p m j r", r=4))
+            elif kind == "xq":
+                a, g = d
                 quant(xcode[(a, g)][:], xscale[(a, g)][:], xb[(a, g)][:].rearrange("p r m j -> p (r m j)"))
-            elif name[0] == "M":
-                g, k = int(name[1]), int(name[3:])
-                a, h, r = BANKS[k]
-                for s in range(2):
-                    nc.tensor.matmul_mx(
-                        out=bank[k % 8][:],
-                        lhsT=xcode[(a, g)][:, P * r : P * (r + 1)].bitcast(FP8X4),
-                        lhsT_scale=xscale[(a, g)][:, P * r : P * (r + 1)],
-                        rhs=wcode[(s, h, g)][:].bitcast(FP8X4),
-                        rhs_scale=wscale[(s, h, g)][:],
-                        start=(g == 0 and s == 0),
-                        stop=(g == 1 and s == 1),
-                    )
-            elif name[0] in "AB":
-                k = int(name[1:])
-                a, h, r = BANKS[k]
-                dst = res[(a, h)][:, r, :]
-                if name[0] == "A" and eng == "V":
-                    nc.vector.tensor_scalar(out=dst, in0=bank[k % 8][:], scalar1=0.0, scalar2=None, op0=ALU.max)
-                elif name[0] == "A":
-                    nc.scalar.activation(out=dst, in_=bank[k % 8][:], func=ACT.Relu)
-                elif eng == "V":
+            elif kind in ("M0", "M1"):
+                a, c0, n, r0 = d
+                cols = slice(P * c0, P * (c0 + n))
+                todo = [(r0, 0)] if kind == "M0" else [(r0, 1)] + [(r, g) for r in range(r0 + 1, r0 + PACK[(a, c0)]) for g in range(2)]
+                for r, g in todo:
+                    for s in range(2):
+                        nc.tensor.matmul_mx(
+                            out=bank[int(arg)][:, P * n * (r - r0) : P * n * (r - r0 + 1)],
+                            lhsT=xcode[(a, g)][:, P * r : P * (r + 1)].bitcast(FP8X4),
+                            lhsT_scale=xscale[(a, g)][:, P * r : P * (r + 1)],
+                            rhs=wcode[(s, g)][:, cols].bitcast(FP8X4),
+                            rhs_scale=wscale[(s, g)][:, cols],
+                            start=(g == 0 and s == 0),
+                            stop=(g == 1 and s == 1),
+                        )
+            elif kind == "A":
+                a, c0, n, r0 = d
+                if (a, c0) not in res:
+                    tile = new("res%d%d" % (a, c0), [P, 4, P * n], F32)
+                    for i in range(n):
+                        res[(a, c0 + i)] = (tile, P * i)
+                nr = PACK[(a, c0)]
+                dst = res[(a, c0)][0][:, r0 : r0 + nr, :].rearrange("p r n -> p (r n)")
+                src = bank[int(arg[1])][:, 0 : P * n * nr]
+                if arg[0] == "V":
+                    nc.vector.tensor_scalar(out=dst, in0=src, scalar1=0.0, scalar2=None, op0=ALU.max)
+                else:
+                    nc.scalar.activation(out=dst, in_=src, func=ACT.Relu)
+            elif kind == "B":
+                a, c0, n, r0, nr = d
+                dst = res[(a, c0)][0][:, r0 : r0 + nr, :].rearrange("p r n -> p (r n)")
+                if arg == "V":
                     nc.vector.tensor_tensor(out=dst, in0=dst, in1=dst, op=ALU.mult)
                 else:
                     nc.scalar.activation(out=dst, in_=dst, func=ACT.Square)
-            elif name[0] in "CQ":
-                a, c = int(name[1]), int(name[2])
-                cols = slice(CH * (c % 2), CH * (c % 2 + 1))
-                if name[0] == "C":
-                    copy(eng, by_runs(ob[(a, c)]), res[(a, c // 2)][:, :, cols].rearrange("p r (c i) -> p c r i", i=2))
-                else:
-                    quant(ocode[(a, c // 2)][:, cols], oscale[a][:, CH * c : CH * (c + 1)], flat(ob[(a, c)]))
-            elif name[:2] == "So":
-                a, h, r = int(name[2]), int(name[3]), int(name[4])
-                nc.sync.dma_start(out=out_rows[a, :, r, 512 * h : 512 * (h + 1)], in_=res[(a, h)][:, r, :])
-            elif name[:2] == "Sw":
-                a, h = int(name[2]), int(name[3])
-                nc.sync.dma_start(out=words_out[a, :, 512 * h : 512 * (h + 1)], in_=ocode[(a, h)][:].bitcast(I32))
+            elif kind == "C":
+                a, c0, n = d
+                ob[(a, c0)] = new("ob" + name, [P, P * n, 4], BF16)
+                t, off = res[(a, c0)]
+                copy(arg, by_runs(ob[(a, c0)]), t[:, :, off : off + P * n].rearrange("p r (c i) -> p c r i", i=2))
+            elif kind == "Q":
+                a, c0, n = d
+                cols = slice(P * c0, P * (c0 + n))
+                quant(ocode[a][:, cols], oscale[4 * a : P, cols], flat(ob[(a, c0)]))
+            elif kind == "So":
+                a, c0, n, r0, nr = d
+                queue.dma_start(out=out_rows[a, :, r0 : r0 + nr, P * c0 : P * (c0 + n)], in_=res[(a, c0)][0][:, r0 : r0 + nr, :])
+            elif kind == "Sw":
+                a, c0, n = d
+                cols = slice(P * c0, P * (c0 + n))
+                queue.dma_start(out=words_out[a, :, cols], in_=ocode[a][:, cols].bitcast(I32))
             else:
-                a = int(name[2])
-                for q in range(4):
-                    nc.sync.dma_start(out=scales_out[a, 4 * q : 4 * q + 4, :], in_=oscale[a][32 * q : 32 * q + 4, :].bitcast(I32))
+                q = d[0]
+                queue.dma_start(out=scales_out[:, 4 * q : 4 * q + 4, :], in_=oscale[32 * q : 32 * q + 8, :].bitcast(I32))

@@ -20,18 +20,17 @@ HI_MASK_PAIR = 0xFFF0FFF0 - (1 << 32)
 PACK = {(0, 0): 1, (0, 4): 2, (0, 6): 2, (1, 0): 1, (1, 4): 2, (1, 6): 2}
 
 ORDER = (
-    "Lw002 Lw022 wc002:V Lw104 wm002 wc022:S wl002 Lx044 wc102:S wm022 Lw042 wc122:S wq002 wl022 wh022 wq022 wm102 "
-    "wh002 Lx144 xc062:S wl102 wm122 wh102 wl122 xc042:S Lw142 wh122 wc042:S Lx004 xq10 M01041:0 Lx104 wq102 "
-    "xc142:S M01042:1 wm042 Lw062 wq122 xc162:V wh042 xq11 M11041:0 M11042:1 M01040:2 wc142:S wl042 A1041:S0 wm142 "
-    "A1042:S1 M11040:2 wq042 M01420:3 wh142 wl142 B10411:S Lw162 xc022:V M01043:4 wq142 xc002:S B10421:S xq00 "
-    "M11043:4 xc102:V M01422:5 xc122:V M11422:5 wc062:V xq01 wm062 M11420:3 So10421 A1040:S2 M00420:6 wc162:V "
-    "M00422:7 M00041:0 A1043:S4 B10401:S A1420:S3 M00040:1 wl062 So10411 M10041:0 wm162 So10401 wq062 B10431:S "
-    "B14202:S wh062 A1422:S5 A0041:S0 B14222:S M00042:2 B00411:S wh162 M00043:4 M10042:2 A0042:S2 So10431 So14202 "
-    "So14222 wl162 M10040:1 M00622:3 C122:V A0040:S1 M10422:7 B00421:S M10043:4 B00401:V M00620:5 wq162 M10420:6 "
-    "M01622:0 A0422:S7 C102:V M11622:0 M10620:5 A0043:S4 M01620:2 B04222:S M10622:3 A0420:V6 M11620:2 B00431:S "
-    "B04202:S Q102 So00411 C142:V A1622:S0 Q122 So00421 Q142 C042:V C022:V A0620:S5 So00401 So04222 So00431 "
-    "B16222:S A0622:V3 B06202:S B06222:S A1620:V2 B16202:S So04202 Sw106 So16222 Q022 C002:V So06202 Q042 So06222 "
-    "Q002 C162:V So16202 C062:S Sw006 Q062 Q162 Sw062 Ssm1 Ssm3:A Ssm2 Ssm0 Sw162:A "
+    "Lw002 Lw022 Lw104 Lx004 Lx104 Lw042 Lx044 Lx144 Lw142 Lw062 Lw162 wc002:V wm002 wh002 wc022:S wl002 wm022 "
+    "wq002 wl022 wc104:S wh022 wq022 xc002:S xc022:V wm104 xq00 wl104 M00040:0 xc102:S M00041:1 xc122:S wj104 "
+    "M00042:2 wc042:S M00043:3 xq01 xc042:S M10040:0 wm042 xc062:V M10041:1 wh042 M10042:2 A0040:S0 xq10 M10043:3 "
+    "A0041:S1 wl042 M01040:4 xc142:S M01041:5 xc162:V M01042:6 A0042:S2 wq042 xq11 M01043:7 A0043:S3 wc142:V "
+    "M00420:0 B00402:S M00422:1 wc062:V M11040:4 wm142 M01420:2 B00422:S wm062 So00402 M11041:5 wl142 M11042:6 "
+    "A1040:S4 So00422 M11043:7 wh142 A1041:S5 wq142 M01422:3 wc162:V A1042:S6 M10420:0 wh062 A1043:S7 wl062 "
+    "M10422:1 B10402:S wm162 M11420:2 wq062 A0420:S0 So10402 wl162 A0422:S1 M01620:4 M11422:3 B04202:S B04222:V "
+    "B10422:S So04202 M00620:5 wh162 So04222 M00622:6 wq162 C042:V M10620:5 A1420:S2 So10422 C004:V A1422:S3 "
+    "M10622:6 B14202:S Q042 B14222:S Q004 M01622:7 So14202 M11620:4 A0620:S5 So14222 C142:V Sw006 A0622:S6 M11622:7 "
+    "C104:V B06202:S B06222:S So06202 Q142 Q104 A1620:S4 So06222 A1622:S7 Sw106 B16202:V B16222:S C062:V So16202 "
+    "So16222:A C162:V Q062 Q162 Sw062 Ssm0:A Ssm1 Ssm2:A Sw162 Ssm3 "
 ).split()
 
 
@@ -45,19 +44,20 @@ def tile_mix_hilo_tm_pl_relu2_kernel(tc, w, x, out_0, out_1, out_2):
         def new(name, shape, dtype):
             return sb.tile(shape, dtype, name=name, align_bytes=256)
 
-        raw, hi, lo, res, ob = {}, {}, {}, {}, {}
+        raw, both, hi, lo, res, ob = {}, {}, {}, {}, {}, {}
         xb = {(a, g): new("xb%d%d" % (a, g), [P, 4, P, 4], BF16) for a in range(2) for g in range(2)}
-        wcode = {(s, g): new("wcode%d%d" % (s, g), [P, M], U32) for s in range(2) for g in range(2)}
-        wscale = {(s, g): new("wscale%d%d" % (s, g), [P, M], U8) for s in range(2) for g in range(2)}
+        wcode = {g: new("wcode%d" % g, [P, 2 * M], U32) for g in range(2)}
+        wscale = {g: new("wscale%d" % g, [P, 2 * M], U8) for g in range(2)}
+
+        def wcols(s, c0, n):
+            first = 1024 * (c0 // 4) + 512 * s + P * (c0 % 4)
+            return slice(first, first + P * n)
+
         xcode = {(a, g): new("xcode%d%d" % (a, g), [P, 512], U32) for a in range(2) for g in range(2)}
         xscale = {(a, g): new("xscale%d%d" % (a, g), [P, 512], U8) for a in range(2) for g in range(2)}
         ocode = {a: new("ocode%d" % a, [P, M], U32) for a in range(2)}
         oscale = new("oscale", [P, M], U8)
         bank = [ps.tile([P, 512], F32, name="bank%d" % i) for i in range(8)]
-
-        warm = new("warm", [P, 8], F32)
-        nc.vector.memset(warm[:], 0.0)
-        nc.scalar.activation(out=warm[:], in_=warm[:], func=ACT.Square)
 
         def copy(eng, out, in_):
             if eng == "V":
@@ -91,16 +91,21 @@ def tile_mix_hilo_tm_pl_relu2_kernel(tc, w, x, out_0, out_1, out_2):
                 nc.sync.dma_start(out=t[:], in_=rows.rearrange("(p j) n -> p j n", j=4))
                 for i in range(n):
                     raw[(kind[1], g, c0 + i)] = (t, P * i)
-            elif kind in ("wc", "wm", "wl", "wh", "wq", "xc"):
+            elif kind in ("wc", "wm", "wl", "wh", "wq", "wj", "xc"):
                 g, c0, n = d
                 t, off = raw[(kind[0], g, c0)]
                 cols = slice(P * c0, P * (c0 + n))
                 key = (g, c0)
                 if kind == "wc":
-                    hi[key] = new("hi" + name, [P, P * n, 4], BF16)
-                    lo[key] = new("lo" + name, [P, P * n, 4], BF16)
+                    both[key] = new("both" + name, [P, 2, P * n, 4], BF16)
+                    hi[key] = both[key][:, 0, :, :]
+                    lo[key] = both[key][:, 1, :, :]
                     upper = t[:].bitcast(BF16)[:, :, 2 * off + 1 : 2 * (off + P * n) : 2]
-                    copy(arg, by_runs(hi[key]), upper.rearrange("p j (c i) -> p c j i", i=2))
+                    upper = upper.rearrange("p j (c i) -> p c j i", i=2)
+                    if arg == "V":
+                        nc.vector.tensor_copy(out=by_runs(hi[key]), in_=upper)
+                    else:
+                        nc.scalar.activation(out=by_runs(hi[key]), in_=upper, func=ACT.Copy)
                 elif kind == "wm":
                     v = flat(hi[key]).bitcast(I32)
                     nc.vector.tensor_scalar(out=v, in0=v, scalar1=HI_MASK_PAIR, scalar2=None, op0=ALU.bitwise_and)
@@ -112,9 +117,11 @@ def tile_mix_hilo_tm_pl_relu2_kernel(tc, w, x, out_0, out_1, out_2):
                         op=ALU.subtract,
                     )
                 elif kind == "wh":
-                    quant(wcode[(0, g)][:, cols], wscale[(0, g)][:, cols], flat(hi[key]))
+                    quant(wcode[g][:, wcols(0, c0, n)], wscale[g][:, wcols(0, c0, n)], flat(hi[key]))
                 elif kind == "wq":
-                    quant(wcode[(1, g)][:, cols], wscale[(1, g)][:, cols], flat(lo[key]))
+                    quant(wcode[g][:, wcols(1, c0, n)], wscale[g][:, wcols(1, c0, n)], flat(lo[key]))
+                elif kind == "wj":
+                    quant(wcode[g][:, wcols(0, c0, 2 * n)], wscale[g][:, wcols(0, c0, 2 * n)], both[key][:].rearrange("p s n j -> p (s n j)"))
                 else:
                     m0 = 32 * (c0 % 4)
                     dst = xb[(c0 // 4, g)][:, :, m0 : m0 + 32 * n, :].rearrange("p r m j -> p m j r")
@@ -132,8 +139,8 @@ def tile_mix_hilo_tm_pl_relu2_kernel(tc, w, x, out_0, out_1, out_2):
                             out=bank[int(arg)][:, P * n * (r - r0) : P * n * (r - r0 + 1)],
                             lhsT=xcode[(a, g)][:, P * r : P * (r + 1)].bitcast(FP8X4),
                             lhsT_scale=xscale[(a, g)][:, P * r : P * (r + 1)],
-                            rhs=wcode[(s, g)][:, cols].bitcast(FP8X4),
-                            rhs_scale=wscale[(s, g)][:, cols],
+                            rhs=wcode[g][:, wcols(s, c0, n)].bitcast(FP8X4),
+                            rhs_scale=wscale[g][:, wcols(s, c0, n)],
                             start=(g == 0 and s == 0),
                             stop=(g == 1 and s == 1),
                         )

from contextlib import ExitStack

import concourse.mybir as mybir

K, M, T = 1024, 1024, 1024
FLOPS = 2 * 2 * K * M * T

F32 = mybir.dt.float32
BF16 = mybir.dt.bfloat16
I32 = mybir.dt.int32
U32 = mybir.dt.uint32
U8 = mybir.dt.uint8
FP8X4 = mybir.dt.float8_e4m3fn_x4
ALU = mybir.AluOpType
ACT = mybir.ActivationFunctionType

P = 128
HI_MASK_PAIR = 0xFFF0FFF0 - (1 << 32)

PACK = {(0, 0): 1, (0, 4): 2, (0, 6): 2, (1, 0): 1, (1, 4): 2, (1, 6): 2}

ORDER = (
    "Lw002 Lw022 Lw104 Lx004 Lx104 Lw042 Lx044 Lx144 Lw142 Lw062 Lw162 wc002:V wm002 wh002 wc022:S wl002 wm022 "
    "wq002 wl022 wc104:S wh022 wq022 xc002:S xc022:V wm104 xq00 wl104 M00040:0 xc102:S M00041:1 xc122:S wj104 "
    "M00042:2 wc042:S M00043:3 xq01 xc042:S M10040:0 wm042 xc062:V M10041:1 wh042 M10042:2 A0040:S0 xq10 M10043:3 "
    "A0041:S1 wl042 M01040:4 xc142:S M01041:5 xc162:V M01042:6 A0042:S2 wq042 xq11 M01043:7 A0043:S3 wc142:V "
    "M00420:0 B00402:S M00422:1 wc062:V M11040:4 wm142 M01420:2 B00422:S wm062 So00402 M11041:5 wl142 M11042:6 "
    "A1040:S4 So00422 M11043:7 wh142 A1041:S5 wq142 M01422:3 wc162:V A1042:S6 M10420:0 wh062 A1043:S7 wl062 "
    "M10422:1 B10402:S wm162 M11420:2 wq062 A0420:S0 So10402 wl162 A0422:S1 M01620:4 M11422:3 B04202:S B04222:V "
    "B10422:S So04202 M00620:5 wh162 So04222 M00622:6 wq162 C042:V M10620:5 A1420:S2 So10422 C004:V A1422:S3 "
    "M10622:6 B14202:S Q042 B14222:S Q004 M01622:7 So14202 M11620:4 A0620:S5 So14222 C142:V Sw006 A0622:S6 M11622:7 "
    "C104:V B06202:S B06222:S So06202 Q142 Q104 A1620:S4 So06222 A1622:S7 Sw106 B16202:V B16222:S C062:V So16202 "
    "So16222:A C162:V Q062 Q162 Sw062 Ssm0:A Ssm1 Ssm2:A Sw162 Ssm3 "
).split()


def tile_mix_hilo_tm_pl_relu2_kernel(tc, w, x, out_0, out_1, out_2):
    nc = tc.nc
    with ExitStack() as ctx:
        sb = ctx.enter_context(tc.tile_pool(name="sb", bufs=1))
        ps = ctx.enter_context(tc.psum_pool(name="ps", bufs=1))
        ctx.enter_context(tc.manual_schedule())

        def new(name, shape, dtype):
            return sb.tile(shape, dtype, name=name, align_bytes=256)

        raw, both, hi, lo, res, ob = {}, {}, {}, {}, {}, {}
        xb = {(a, g): new("xb%d%d" % (a, g), [P, 4, P, 4], BF16) for a in range(2) for g in range(2)}
        wcode = {g: new("wcode%d" % g, [P, 2 * M], U32) for g in range(2)}
        wscale = {g: new("wscale%d" % g, [P, 2 * M], U8) for g in range(2)}

        def wcols(s, c0, n):
            first = 1024 * (c0 // 4) + 512 * s + P * (c0 % 4)
            return slice(first, first + P * n)

        xcode = {(a, g): new("xcode%d%d" % (a, g), [P, 512], U32) for a in range(2) for g in range(2)}
        xscale = {(a, g): new("xscale%d%d" % (a, g), [P, 512], U8) for a in range(2) for g in range(2)}
        ocode = {a: new("ocode%d" % a, [P, M], U32) for a in range(2)}
        oscale = new("oscale", [P, M], U8)
        bank = [ps.tile([P, 512], F32, name="bank%d" % i) for i in range(8)]

        def copy(eng, out, in_):
            if eng == "V":
                nc.vector.tensor_copy(out=out, in_=in_)
            else:
                nc.scalar.copy(out=out, in_=in_)

        def quant(codes, scales, src):
            nc.vector.quantize_mx(out=codes.bitcast(FP8X4), scales=scales, in_=src)

        def flat(t):
            return t[:].rearrange("p n j -> p (n j)")

        def by_runs(t):
            return t[:].rearrange("p (c i) j -> p c j i", i=2)

        out_rows = out_0.rearrange("(a p r) n -> a p r n", a=2, r=4)
        words_out = out_1.rearrange("a p n i -> a p (n i)").bitcast(I32)
        scales_out = out_2.bitcast(I32)

        for step in ORDER:
            name, arg = (step.split(":") + [""])[:2]
            kind = name[:2] if name[0] in "LwxMS" else name[0]
            d = [int(ch) for ch in name[len(kind) :] if ch in "0123456789"]
            queue = nc.scalar if arg == "A" else nc.sync
            if kind[0] == "L":
                g, c0, n = d
                src = w if kind == "Lw" else x
                t = new("raw" + name, [P, 4, P * n], F32)
                rows = src[512 * g : 512 * (g + 1), P * c0 : P * (c0 + n)]
                nc.sync.dma_start(out=t[:], in_=rows.rearrange("(p j) n -> p j n", j=4))
                for i in range(n):
                    raw[(kind[1], g, c0 + i)] = (t, P * i)
            elif kind in ("wc", "wm", "wl", "wh", "wq", "wj", "xc"):
                g, c0, n = d
                t, off = raw[(kind[0], g, c0)]
                cols = slice(P * c0, P * (c0 + n))
                key = (g, c0)
                if kind == "wc":
                    both[key] = new("both" + name, [P, 2, P * n, 4], BF16)
                    hi[key] = both[key][:, 0, :, :]
                    lo[key] = both[key][:, 1, :, :]
                    upper = t[:].bitcast(BF16)[:, :, 2 * off + 1 : 2 * (off + P * n) : 2]
                    upper = upper.rearrange("p j (c i) -> p c j i", i=2)
                    if arg == "V":
                        nc.vector.tensor_copy(out=by_runs(hi[key]), in_=upper)
                    else:
                        nc.scalar.activation(out=by_runs(hi[key]), in_=upper, func=ACT.Copy)
                elif kind == "wm":
                    v = flat(hi[key]).bitcast(I32)
                    nc.vector.tensor_scalar(out=v, in0=v, scalar1=HI_MASK_PAIR, scalar2=None, op0=ALU.bitwise_and)
                elif kind == "wl":
                    nc.vector.tensor_tensor(
                        out=by_runs(lo[key]),
                        in0=t[:, :, off : off + P * n].rearrange("p j (c i) -> p c j i", i=2),
                        in1=by_runs(hi[key]),
                        op=ALU.subtract,
                    )
                elif kind == "wh":
                    quant(wcode[g][:, wcols(0, c0, n)], wscale[g][:, wcols(0, c0, n)], flat(hi[key]))
                elif kind == "wq":
                    quant(wcode[g][:, wcols(1, c0, n)], wscale[g][:, wcols(1, c0, n)], flat(lo[key]))
                elif kind == "wj":
                    quant(wcode[g][:, wcols(0, c0, 2 * n)], wscale[g][:, wcols(0, c0, 2 * n)], both[key][:].rearrange("p s n j -> p (s n j)"))
                else:
                    m0 = 32 * (c0 % 4)
                    dst = xb[(c0 // 4, g)][:, :, m0 : m0 + 32 * n, :].rearrange("p r m j -> p m j r")
                    copy(arg, dst, t[:, :, off : off + P * n].rearrange("p j (m r) -> p m j r", r=4))
            elif kind == "xq":
                a, g = d
                quant(xcode[(a, g)][:], xscale[(a, g)][:], xb[(a, g)][:].rearrange("p r m j -> p (r m j)"))
            elif kind in ("M0", "M1"):
                a, c0, n, r0 = d
                cols = slice(P * c0, P * (c0 + n))
                todo = [(r0, 0)] if kind == "M0" else [(r0, 1)] + [(r, g) for r in range(r0 + 1, r0 + PACK[(a, c0)]) for g in range(2)]
                for r, g in todo:
                    for s in range(2):
                        nc.tensor.matmul_mx(
                            out=bank[int(arg)][:, P * n * (r - r0) : P * n * (r - r0 + 1)],
                            lhsT=xcode[(a, g)][:, P * r : P * (r + 1)].bitcast(FP8X4),
                            lhsT_scale=xscale[(a, g)][:, P * r : P * (r + 1)],
                            rhs=wcode[g][:, wcols(s, c0, n)].bitcast(FP8X4),
                            rhs_scale=wscale[g][:, wcols(s, c0, n)],
                            start=(g == 0 and s == 0),
                            stop=(g == 1 and s == 1),
                        )
            elif kind == "A":
                a, c0, n, r0 = d
                if (a, c0) not in res:
                    tile = new("res%d%d" % (a, c0), [P, 4, P * n], F32)
                    for i in range(n):
                        res[(a, c0 + i)] = (tile, P * i)
                nr = PACK[(a, c0)]
                dst = res[(a, c0)][0][:, r0 : r0 + nr, :].rearrange("p r n -> p (r n)")
                src = bank[int(arg[1])][:, 0 : P * n * nr]
                if arg[0] == "V":
                    nc.vector.tensor_scalar(out=dst, in0=src, scalar1=0.0, scalar2=None, op0=ALU.max)
                else:
                    nc.scalar.activation(out=dst, in_=src, func=ACT.Relu)
            elif kind == "B":
                a, c0, n, r0, nr = d
                dst = res[(a, c0)][0][:, r0 : r0 + nr, :].rearrange("p r n -> p (r n)")
                if arg == "V":
                    nc.vector.tensor_tensor(out=dst, in0=dst, in1=dst, op=ALU.mult)
                else:
                    nc.scalar.activation(out=dst, in_=dst, func=ACT.Square)
            elif kind == "C":
                a, c0, n = d
                ob[(a, c0)] = new("ob" + name, [P, P * n, 4], BF16)
                t, off = res[(a, c0)]
                copy(arg, by_runs(ob[(a, c0)]), t[:, :, off : off + P * n].rearrange("p r (c i) -> p c r i", i=2))
            elif kind == "Q":
                a, c0, n = d
                cols = slice(P * c0, P * (c0 + n))
                quant(ocode[a][:, cols], oscale[4 * a : P, cols], flat(ob[(a, c0)]))
            elif kind == "So":
                a, c0, n, r0, nr = d
                queue.dma_start(out=out_rows[a, :, r0 : r0 + nr, P * c0 : P * (c0 + n)], in_=res[(a, c0)][0][:, r0 : r0 + nr, :])
            elif kind == "Sw":
                a, c0, n = d
                cols = slice(P * c0, P * (c0 + n))
                queue.dma_start(out=words_out[a, :, cols], in_=ocode[a][:, cols].bitcast(I32))
            else:
                q = d[0]
                queue.dma_start(out=scales_out[:, 4 * q : 4 * q + 4, :], in_=oscale[32 * q : 32 * q + 8, :].bitcast(I32))
